import numpy as np
CORES = [2,10,18,26,34,42,50,58,130,138,146,154,162,170,178,186]
N = 16
ROUNDS, ROOT = 8, 5
DEAD = {"mate_links":[[4,0]],"switch_ports":[[5,0],[5,1]],"chips":[]}
def setup_inputs(rng):
    return {"x": rng.standard_normal((N, ROUNDS, 128, 128), dtype=np.float32)}
def reference(x):
    y = np.full(x.shape, np.nan, x.dtype)
    y[ROOT] = x.sum(axis=0, dtype=np.float64).astype(x.dtype)
    return {"y": y}

@@ -1,0 +1,48 @@
+from concourse.mybir import AluOpType
+
+SCRATCH = {
+    "slot": ("dram", [128, 512], "float32"),
+}
+SEMAPHORES = ["ld", "arr", "sent", "cred"]
+
+ORDER = [138, 130, 146, 154, 170, 162, 178, 186, 58, 50, 18, 26, 10, 2, 34, 42]
+ENG = 0xFF
+
+
+def rank_program(g, core, T, topo):
+    if T.rank_of(core) is None:
+        return
+    i = ORDER.index(core)
+    prev = ORDER[i - 1] if i > 0 else None
+    nxt = ORDER[i + 1] if i + 1 < len(ORDER) else None
+    ld = 0
+    sent = 0
+    if nxt is None:
+        g.dma_start(T.y[:], T.x[:]).then_inc(T.sem.ld, 16)
+        ld += 16
+        g.wait_ge(T.sem.ld, ld)
+    for gen in range(2):
+        xs = T.x[4 * gen:4 * gen + 4]
+        if prev is None:
+            g.dma_start(T.slot[:], xs).then_inc(T.sem.ld, 16)
+        else:
+            g.wait_ge(T.sem.arr, 8 * (gen + 1))
+            if nxt is None:
+                g.dma_start(T.y[4 * gen:4 * gen + 4], T.slot[:], accum_op=AluOpType.add,
+                            max_dma_last_dim=8192).then_inc(T.sem.ld, 16)
+            else:
+                g.dma_start(T.slot[:], xs, accum_op=AluOpType.add, max_dma_last_dim=8192).then_inc(T.sem.ld, 16)
+        ld += 16
+        g.wait_ge(T.sem.ld, ld)
+        if nxt is not None:
+            if gen == 1:
+                g.wait_ge(T.sem.cred, 1)
+            rid, pid = topo.addr(nxt, core)
+            g.remote_dma(T.slot[:], T.slot[:], T.sem.arr, T.sem.sent, pid, rid, ENG)
+            sent += 8
+            g.wait_ge(T.sem.sent, sent)
+        if prev is not None and gen == 0:
+            rid, pid = topo.addr(prev, core)
+            g.remote_sem_update(T.sem.cred, T.sem.sent, pid, rid, 0x01)
+            sent += 1
+            g.wait_ge(T.sem.sent, sent)

@@ -1,48 +1,189 @@
+from concourse.bass import DstId, RemoteDMATransfer
 from concourse.mybir import AluOpType
 
 SCRATCH = {
-    "slot": ("dram", [128, 512], "float32"),
+    "buf": ("dram", [2, 128, 256], "float32"),
 }
-SEMAPHORES = ["ld", "arr", "sent", "cred"]
+SEMAPHORES = ["ld", "sent", "arr0", "arr1", "crA", "crB"]
 
-ORDER = [138, 130, 146, 154, 170, 162, 178, 186, 58, 50, 18, 26, 10, 2, 34, 42]
-ENG = 0xFF
+RING = [16, 17, 19, 18, 20, 21, 23, 22]
+PATH = [0, 2, 3, 1, 7, 6]
+GATE, ROOT = 4, 5
+DATA_ENGINES = 0xFF
+SIGNAL_ENGINE = 0x01
+
+
+def world(chip):
+    return (chip // 16) * 128 + (chip % 16) * 8 + 2
+
+
+def build():
+    a1, a2, a3, a4, e, b3, b2, b1 = RING
+    par = [{}, {}]
+
+    def link(f, seq):
+        for i in range(len(seq) - 1):
+            par[f][seq[i]] = seq[i + 1]
+
+    link(0, [a1, a2, a3, a4, e, PATH[5]])
+    link(0, [b1, b2, b3, e])
+    link(0, PATH + [GATE, ROOT])
+    link(1, [e, b3, b2, b1, a1, PATH[0]])
+    link(1, [a4, a3, a2, a1])
+    link(1, PATH[::-1] + [GATE, ROOT])
+    chips = RING + PATH + [GATE, ROOT]
+    kids = [{v: [c for c in chips if par[f].get(c) == v] for v in chips} for f in (0, 1)]
+    both = {a2: 0, b3: 1}
+
+    slot = {}
+    tenants = {}
+    for v in chips:
+        first = both.get(v, 0)
+        for f in (0, 1):
+            if v != ROOT and not kids[f][v]:
+                first = f
+        for f in (first, 1 - first):
+            for j in (0, 1):
+                for c in (kids[f][v] or [None]):
+                    s = f
+                    if v in both:
+                        s = j
+                    elif c is not None and len(kids[f][v]) == 2 and par[1 - f][v] == c:
+                        s = 1 - f
+                    slot[(v, f, j, c)] = s
+                    tenants.setdefault((v, s), []).append((f, j, c))
+
+    need = {}
+    after = {}
+    ncred = {}
+
+    def dep(op, what, on):
+        need.setdefault(op, []).append(what)
+        after.setdefault(op, []).append(on)
+
+    for (v, s), seq in sorted(tenants.items()):
+        landed = 0
+        count = {}
+        for i, (f, j, c) in enumerate(seq):
+            if c is not None:
+                landed += 8
+                count[i] = landed
+        for i, (f, j, c) in enumerate(seq):
+            before = seq[i - 1] if i else None
+            if c is None:
+                need.setdefault(('D', v, f, j), [])
+                after.setdefault(('D', v, f, j), [])
+                if before:
+                    dep(('D', v, f, j), ('sent',), ('D', v, before[0], before[1]))
+                continue
+            if v != ROOT:
+                dep(('D', v, f, j), ('arr', s, count[i]), ('D', c, f, j))
+            if not before:
+                continue
+            reader = ('D', v, before[0], before[1])
+            if v != ROOT and par[before[0]][v] == c:
+                sc = slot[(c, before[0], before[1], v)]
+                k = tenants[(c, sc)].index((before[0], before[1], v))
+                n = 8 * len([t for t in tenants[(c, sc)][:k + 1] if t[2] is not None])
+                dep(('D', c, f, j), ('arr', sc, n), reader)
+            elif v == ROOT:
+                sig = ('K', v, c, 0, j)
+                dep(('D', c, f, j), ('cr', 0, 1), sig)
+                dep(sig, ('ld',), ('D', c, before[0], before[1]))
+            else:
+                sig = ('K', v, c, f, j)
+                ncred[(c, f)] = ncred.get((c, f), 0) + 1
+                dep(('D', c, f, j), ('cr', f, ncred[(c, f)]), sig)
+                dep(sig, ('sent',), reader)
+
+    depth = {}
+
+    def deep(op):
+        if op not in depth:
+            depth[op] = 1 + max([deep(o) for o in after[op]] + [0])
+        return depth[op]
+
+    for op in list(after):
+        deep(op)
+    return par, kids, slot, need, depth
 
 
 def rank_program(g, core, T, topo):
     if T.rank_of(core) is None:
         return
-    i = ORDER.index(core)
-    prev = ORDER[i - 1] if i > 0 else None
-    nxt = ORDER[i + 1] if i + 1 < len(ORDER) else None
-    ld = 0
-    sent = 0
-    if nxt is None:
-        g.dma_start(T.y[:], T.x[:]).then_inc(T.sem.ld, 16)
-        ld += 16
-        g.wait_ge(T.sem.ld, ld)
-    for gen in range(2):
-        xs = T.x[4 * gen:4 * gen + 4]
-        if prev is None:
-            g.dma_start(T.slot[:], xs).then_inc(T.sem.ld, 16)
+    par, kids, slot, need, depth = build()
+    me = 16 * topo.host(core) + topo.chip(core)
+    arr = [T.sem.arr0, T.sem.arr1]
+    cr = [T.sem.crA, T.sem.crB]
+    n = {"ld": 0, "sent": 0}
+    seen = {}
+
+    def wait(key, sem, count):
+        if seen.get(key, 0) < count:
+            g.wait_ge(sem, count)
+            seen[key] = count
+
+    def local(out, in_, add):
+        if add:
+            g.dma_start(out, in_, accum_op=AluOpType.add, max_dma_last_dim=8192).then_inc(T.sem.ld, 16)
         else:
-            g.wait_ge(T.sem.arr, 8 * (gen + 1))
-            if nxt is None:
-                g.dma_start(T.y[4 * gen:4 * gen + 4], T.slot[:], accum_op=AluOpType.add,
-                            max_dma_last_dim=8192).then_inc(T.sem.ld, 16)
+            g.dma_start(out, in_).then_inc(T.sem.ld, 16)
+        n["ld"] += 16
+
+    def signal(chip, f):
+        rid, pid = topo.addr(world(chip), core)
+        g.remote_sem_update(cr[f], T.sem.sent, pid, rid, SIGNAL_ENGINE)
+        n["sent"] += 1
+
+    if me == ROOT:
+        local(T.y[:], T.x[:], False)
+        for j in (0, 1):
+            wait("arr0", arr[0], 8 * (j + 1))
+            wait("arr1", arr[1], 8 * (j + 1))
+            wait("ld", T.sem.ld, n["ld"])
+            local(T.y[4 * j:4 * j + 4], T.buf[:], True)
+            wait("ld", T.sem.ld, n["ld"])
+            if j == 0:
+                signal(GATE, 0)
+        wait("sent", T.sem.sent, n["sent"])
+        return
+
+    mine = sorted((d, op) for op, d in depth.items() if op[1] == me)
+    for t in sorted({d for d, op in mine}):
+        ops = [op for d, op in mine if d == t]
+        data = [op for op in ops if op[0] == 'D']
+        todo = [w for op in ops for w in need[op]]
+        if ('sent',) in todo:
+            wait("sent", T.sem.sent, n["sent"])
+        for w in todo:
+            if w[0] == 'arr':
+                wait("arr%d" % w[1], arr[w[1]], w[2])
+        for (k, v, f, j) in data:
+            xs = T.x[4 * j + 2 * f:4 * j + 2 * f + 2]
+            cs = kids[f][me]
+            if cs:
+                local(T.buf[slot[(me, f, j, cs[0])]], xs, True)
             else:
-                g.dma_start(T.slot[:], xs, accum_op=AluOpType.add, max_dma_last_dim=8192).then_inc(T.sem.ld, 16)
-        ld += 16
-        g.wait_ge(T.sem.ld, ld)
-        if nxt is not None:
-            if gen == 1:
-                g.wait_ge(T.sem.cred, 1)
-            rid, pid = topo.addr(nxt, core)
-            g.remote_dma(T.slot[:], T.slot[:], T.sem.arr, T.sem.sent, pid, rid, ENG)
-            sent += 8
-            g.wait_ge(T.sem.sent, sent)
-        if prev is not None and gen == 0:
-            rid, pid = topo.addr(prev, core)
-            g.remote_sem_update(T.sem.cred, T.sem.sent, pid, rid, 0x01)
-            sent += 1
-            g.wait_ge(T.sem.sent, sent)
+                local(T.buf[slot[(me, f, j, None)]], xs, False)
+        for w in todo:
+            if w[0] == 'cr':
+                wait("cr%d" % w[1], cr[w[1]], w[2])
+        wait("ld", T.sem.ld, n["ld"])
+        for (k, v, f, j) in data:
+            p = par[f][me]
+            rid, pid = topo.addr(world(p), core)
+            dst = T.buf[slot[(p, f, j, me)]]
+            cs = kids[f][me]
+            if len(cs) == 2:
+                g.remote_dma_fused([RemoteDMATransfer(
+                    dst_ids=[DstId(rid=rid, pnc=pid)], dma_engine_mask=DATA_ENGINES,
+                    remote_sem=arr[slot[(p, f, j, me)]],
+                    srcs=[T.buf[slot[(me, f, j, c)]] for c in cs], dsts=[dst], alu_op=1)], local_sem=T.sem.sent)
+            else:
+                src = T.buf[slot[(me, f, j, cs[0] if cs else None)]]
+                g.remote_dma(dst, src, arr[slot[(p, f, j, me)]], T.sem.sent, pid, rid, DATA_ENGINES)
+            n["sent"] += 8
+        for op in ops:
+            if op[0] == 'K':
+                signal(op[2], op[3])
+    wait("sent", T.sem.sent, n["sent"])

@@ -9,8 +9,9 @@ SEMAPHORES = ["ld", "sent", "arr0", "arr1", "crA", "crB"]
 RING = [16, 17, 19, 18, 20, 21, 23, 22]
 PATH = [0, 2, 3, 1, 7, 6]
 GATE, ROOT = 4, 5
+CROSS = {(19, 0), (19, 1), (23, 0), (23, 1), (18, 0), (22, 1),
+         (3, 0), (3, 1), (1, 0), (1, 1), (2, 1), (7, 0)}
 DATA_ENGINES = 0xFF
-SIGNAL_ENGINE = 0x01
 
 
 def world(chip):
@@ -38,20 +39,22 @@ def build():
     slot = {}
     tenants = {}
     for v in chips:
-        first = both.get(v, 0)
+        late = 0 if (v, 0) in CROSS else 1
+        order = [(0, 0), (1, 0), (1 - late, 1), (late, 1)]
         for f in (0, 1):
-            if v != ROOT and not kids[f][v]:
-                first = f
-        for f in (first, 1 - first):
-            for j in (0, 1):
-                for c in (kids[f][v] or [None]):
-                    s = f
-                    if v in both:
-                        s = j
-                    elif c is not None and len(kids[f][v]) == 2 and par[1 - f][v] == c:
-                        s = 1 - f
-                    slot[(v, f, j, c)] = s
-                    tenants.setdefault((v, s), []).append((f, j, c))
+            if both.get(v) == f or (v != ROOT and not kids[f][v]):
+                order = [(f, 0), (f, 1), (1 - f, 0), (1 - f, 1)]
+        for f, j in order:
+            for c in (kids[f][v] or [None]):
+                s = f
+                if v in both:
+                    s = j
+                elif c is not None and len(kids[f][v]) == 2 and par[1 - f][v] == c:
+                    s = 1 - f
+                elif c is not None and j == 1 and (v, f) in CROSS:
+                    s = 1 - f
+                slot[(v, f, j, c)] = s
+                tenants.setdefault((v, s), []).append((f, j, c))
 
     need = {}
     after = {}
@@ -130,10 +133,13 @@ def rank_program(g, core, T, topo):
             g.dma_start(out, in_).then_inc(T.sem.ld, 16)
         n["ld"] += 16
 
-    def signal(chip, f):
-        rid, pid = topo.addr(world(chip), core)
-        g.remote_sem_update(cr[f], T.sem.sent, pid, rid, SIGNAL_ENGINE)
-        n["sent"] += 1
+    def signal(targets):
+        trs = []
+        for i, (chip, f) in enumerate(targets):
+            rid, pid = topo.addr(world(chip), core)
+            trs.append(RemoteDMATransfer(dst_ids=[DstId(rid=rid, pnc=pid)], dma_engine_mask=1 << i, remote_sem=cr[f]))
+        g.remote_dma_fused(trs, local_sem=T.sem.sent)
+        n["sent"] += len(targets)
 
     if me == ROOT:
         local(T.y[:], T.x[:], False)
@@ -144,7 +150,7 @@ def rank_program(g, core, T, topo):
             local(T.y[4 * j:4 * j + 4], T.buf[:], True)
             wait("ld", T.sem.ld, n["ld"])
             if j == 0:
-                signal(GATE, 0)
+                signal([(GATE, 0)])
         wait("sent", T.sem.sent, n["sent"])
         return
 
@@ -183,7 +189,7 @@ def rank_program(g, core, T, topo):
                 src = T.buf[slot[(me, f, j, cs[0] if cs else None)]]
                 g.remote_dma(dst, src, arr[slot[(p, f, j, me)]], T.sem.sent, pid, rid, DATA_ENGINES)
             n["sent"] += 8
-        for op in ops:
-            if op[0] == 'K':
-                signal(op[2], op[3])
+        sigs = [(op[2], op[3]) for op in ops if op[0] == 'K']
+        if sigs:
+            signal(sigs)
     wait("sent", T.sem.sent, n["sent"])

@@ -4,18 +4,31 @@ from concourse.mybir import AluOpType
 SCRATCH = {
     "buf": ("dram", [2, 128, 256], "float32"),
 }
-SEMAPHORES = ["ld", "sent", "arr0", "arr1", "crA", "crB"]
+SEMAPHORES = ["ld0", "ld1", "sent", "arr0", "arr1", "crA", "crB"]
 
 RING = [16, 17, 19, 18, 20, 21, 23, 22]
 PATH = [0, 2, 3, 1, 7, 6]
 GATE, ROOT = 4, 5
 CROSS = {(19, 0), (19, 1), (23, 0), (23, 1), (18, 0), (22, 1),
          (3, 0), (3, 1), (1, 0), (1, 1), (2, 1), (7, 0)}
+ADD_TO = {16: 17, 20: 21, 0: 16, 6: 20}
 DATA_ENGINES = 0xFF
+DIE = 1
 
 
 def world(chip):
     return (chip // 16) * 128 + (chip % 16) * 8 + 2
+
+
+def alive(src, dst, dead):
+    at = src
+    if (src ^ dst) & 1:
+        if [src, DIE] in dead["mate_links"] or [src ^ 1, DIE] in dead["mate_links"] or (src ^ 1) in dead["chips"]:
+            return False
+        at = src ^ 1
+    if at != dst and ([at, DIE] in dead["switch_ports"] or [dst, DIE] in dead["switch_ports"]):
+        return False
+    return dst not in dead["chips"]
 
 
 def build():
@@ -34,6 +47,9 @@ def build():
     link(1, PATH[::-1] + [GATE, ROOT])
     chips = RING + PATH + [GATE, ROOT]
     kids = [{v: [c for c in chips if par[f].get(c) == v] for v in chips} for f in (0, 1)]
+    for f in (0, 1):
+        for v in chips:
+            kids[f][v].sort(key=lambda c: c != ADD_TO.get(v))
     both = {a2: 0, b3: 1}
 
     slot = {}
@@ -66,22 +82,23 @@ def build():
 
     for (v, s), seq in sorted(tenants.items()):
         landed = 0
-        count = {}
-        for i, (f, j, c) in enumerate(seq):
-            if c is not None:
-                landed += 8
-                count[i] = landed
+        loaded = 0
         for i, (f, j, c) in enumerate(seq):
             before = seq[i - 1] if i else None
-            if c is None:
-                need.setdefault(('D', v, f, j), [])
-                after.setdefault(('D', v, f, j), [])
-                if before:
-                    dep(('D', v, f, j), ('sent',), ('D', v, before[0], before[1]))
-                continue
-            if v != ROOT:
-                dep(('D', v, f, j), ('arr', s, count[i]), ('D', c, f, j))
-            if not before:
+            if c is not None:
+                landed += 8
+            if v != ROOT and (c is None or c == kids[f][v][0]):
+                loaded += 16
+                need.setdefault(('L', v, f, j), [])
+                after.setdefault(('L', v, f, j), [])
+                dep(('D', v, f, j), ('ld', s, loaded), ('L', v, f, j))
+                if c is not None:
+                    dep(('L', v, f, j), ('arr', s, landed), ('D', c, f, j))
+                elif before:
+                    dep(('L', v, f, j), ('sent',), ('D', v, before[0], before[1]))
+            elif v != ROOT:
+                dep(('D', v, f, j), ('arr', s, landed), ('D', c, f, j))
+            if c is None or not before:
                 continue
             reader = ('D', v, before[0], before[1])
             if v != ROOT and par[before[0]][v] == c:
@@ -92,33 +109,36 @@ def build():
             elif v == ROOT:
                 sig = ('K', v, c, 0, j)
                 dep(('D', c, f, j), ('cr', 0, 1), sig)
-                dep(sig, ('ld',), ('D', c, before[0], before[1]))
+                dep(sig, ('root',), ('D', c, before[0], before[1]))
             else:
                 sig = ('K', v, c, f, j)
                 ncred[(c, f)] = ncred.get((c, f), 0) + 1
                 dep(('D', c, f, j), ('cr', f, ncred[(c, f)]), sig)
                 dep(sig, ('sent',), reader)
 
-    depth = {}
+    ready = {}
 
-    def deep(op):
-        if op not in depth:
-            depth[op] = 1 + max([deep(o) for o in after[op]] + [0])
-        return depth[op]
+    def chain(op):
+        if op not in ready:
+            got = [chain(o) for o in after[op]] + [(0, 0)]
+            ready[op] = (max(w for w, s in got), max(s for w, s in got) + (1 if op[1] == ROOT else 0))
+        w, s = ready[op]
+        return (w + (op[0] != 'L'), s + 1)
 
     for op in list(after):
-        deep(op)
-    return par, kids, slot, need, depth
+        chain(op)
+    return par, kids, slot, need, ready
 
 
 def rank_program(g, core, T, topo):
     if T.rank_of(core) is None:
         return
-    par, kids, slot, need, depth = build()
+    par, kids, slot, need, ready = build()
     me = 16 * topo.host(core) + topo.chip(core)
     arr = [T.sem.arr0, T.sem.arr1]
     cr = [T.sem.crA, T.sem.crB]
-    n = {"ld": 0, "sent": 0}
+    ld = [T.sem.ld0, T.sem.ld1]
+    n = {"sent": 0}
     seen = {}
 
     def wait(key, sem, count):
@@ -126,70 +146,70 @@ def rank_program(g, core, T, topo):
             g.wait_ge(sem, count)
             seen[key] = count
 
-    def local(out, in_, add):
+    def local(out, in_, add, sem):
         if add:
-            g.dma_start(out, in_, accum_op=AluOpType.add, max_dma_last_dim=8192).then_inc(T.sem.ld, 16)
+            g.dma_start(out, in_, accum_op=AluOpType.add, max_dma_last_dim=8192).then_inc(sem, 16)
         else:
-            g.dma_start(out, in_).then_inc(T.sem.ld, 16)
-        n["ld"] += 16
+            g.dma_start(out, in_).then_inc(sem, 16)
+
+    def address(chip):
+        if not alive(me, chip, T.tables["DEAD"]):
+            raise ValueError("the plan's write from chip %d to chip %d crosses a dead part" % (me, chip))
+        return topo.addr(world(chip), core)
 
     def signal(targets):
         trs = []
         for i, (chip, f) in enumerate(targets):
-            rid, pid = topo.addr(world(chip), core)
+            rid, pid = address(chip)
             trs.append(RemoteDMATransfer(dst_ids=[DstId(rid=rid, pnc=pid)], dma_engine_mask=1 << i, remote_sem=cr[f]))
         g.remote_dma_fused(trs, local_sem=T.sem.sent)
         n["sent"] += len(targets)
 
     if me == ROOT:
-        local(T.y[:], T.x[:], False)
+        local(T.y[:], T.x[:], False, ld[0])
+        wait("ld0", ld[0], 16)
         for j in (0, 1):
             wait("arr0", arr[0], 8 * (j + 1))
             wait("arr1", arr[1], 8 * (j + 1))
-            wait("ld", T.sem.ld, n["ld"])
-            local(T.y[4 * j:4 * j + 4], T.buf[:], True)
-            wait("ld", T.sem.ld, n["ld"])
+            local(T.y[4 * j:4 * j + 4], T.buf[:], True, ld[0])
+            wait("ld0", ld[0], 16 * (j + 2))
             if j == 0:
                 signal([(GATE, 0)])
         wait("sent", T.sem.sent, n["sent"])
         return
 
-    mine = sorted((d, op) for op, d in depth.items() if op[1] == me)
-    for t in sorted({d for d, op in mine}):
-        ops = [op for d, op in mine if d == t]
-        data = [op for op in ops if op[0] == 'D']
-        todo = [w for op in ops for w in need[op]]
-        if ('sent',) in todo:
+    mine = sorted((r, op) for op, r in ready.items() if op[1] == me)
+    for t in sorted({r[0] for r, op in mine}):
+        ops = [op for r, op in mine if r[0] == t]
+        if [op for op in ops if ('sent',) in need[op]]:
             wait("sent", T.sem.sent, n["sent"])
-        for w in todo:
-            if w[0] == 'arr':
-                wait("arr%d" % w[1], arr[w[1]], w[2])
-        for (k, v, f, j) in data:
-            xs = T.x[4 * j + 2 * f:4 * j + 2 * f + 2]
-            cs = kids[f][me]
-            if cs:
-                local(T.buf[slot[(me, f, j, cs[0])]], xs, True)
-            else:
-                local(T.buf[slot[(me, f, j, None)]], xs, False)
-        for w in todo:
-            if w[0] == 'cr':
-                wait("cr%d" % w[1], cr[w[1]], w[2])
-        wait("ld", T.sem.ld, n["ld"])
-        for (k, v, f, j) in data:
-            p = par[f][me]
-            rid, pid = topo.addr(world(p), core)
-            dst = T.buf[slot[(p, f, j, me)]]
-            cs = kids[f][me]
-            if len(cs) == 2:
-                g.remote_dma_fused([RemoteDMATransfer(
-                    dst_ids=[DstId(rid=rid, pnc=pid)], dma_engine_mask=DATA_ENGINES,
-                    remote_sem=arr[slot[(p, f, j, me)]],
-                    srcs=[T.buf[slot[(me, f, j, c)]] for c in cs], dsts=[dst], alu_op=1)], local_sem=T.sem.sent)
-            else:
-                src = T.buf[slot[(me, f, j, cs[0] if cs else None)]]
-                g.remote_dma(dst, src, arr[slot[(p, f, j, me)]], T.sem.sent, pid, rid, DATA_ENGINES)
-            n["sent"] += 8
         sigs = [(op[2], op[3]) for op in ops if op[0] == 'K']
         if sigs:
             signal(sigs)
+        for op in ops:
+            if op[0] == 'K':
+                continue
+            for w in need[op]:
+                if w[0] == 'arr':
+                    wait("arr%d" % w[1], arr[w[1]], w[2])
+                elif w[0] == 'cr':
+                    wait("cr%d" % w[1], cr[w[1]], w[2])
+                elif w[0] == 'ld':
+                    wait("ld%d" % w[1], ld[w[1]], w[2])
+            k, v, f, j = op
+            cs = kids[f][me]
+            mine_in = [slot[(me, f, j, c)] for c in (cs or [None])]
+            if k == 'L':
+                local(T.buf[mine_in[0]], T.x[4 * j + 2 * f:4 * j + 2 * f + 2], bool(cs), ld[mine_in[0]])
+                continue
+            p = par[f][me]
+            s = slot[(p, f, j, me)]
+            rid, pid = address(p)
+            if len(cs) == 2:
+                g.remote_dma_fused([RemoteDMATransfer(
+                    dst_ids=[DstId(rid=rid, pnc=pid)], dma_engine_mask=DATA_ENGINES, remote_sem=arr[s],
+                    srcs=[T.buf[i] for i in mine_in], dsts=[T.buf[s]], alu_op=1)], local_sem=T.sem.sent)
+            else:
+                g.remote_dma(T.buf[s], T.buf[mine_in[0]], arr[s], T.sem.sent, pid, rid, DATA_ENGINES)
+            n["sent"] += 8
     wait("sent", T.sem.sent, n["sent"])

from concourse.bass import DstId, RemoteDMATransfer
from concourse.mybir import AluOpType

SCRATCH = {
    "buf": ("dram", [2, 128, 256], "float32"),
}
SEMAPHORES = ["ld0", "ld1", "sent", "arr0", "arr1", "crA", "crB"]

RING = [16, 17, 19, 18, 20, 21, 23, 22]
PATH = [0, 2, 3, 1, 7, 6]
GATE, ROOT = 4, 5
CROSS = {(19, 0), (19, 1), (23, 0), (23, 1), (18, 0), (22, 1),
         (3, 0), (3, 1), (1, 0), (1, 1), (2, 1), (7, 0)}
ADD_TO = {16: 17, 20: 21, 0: 16, 6: 20}
DATA_ENGINES = 0xFF
DIE = 1


def world(chip):
    return (chip // 16) * 128 + (chip % 16) * 8 + 2


def alive(src, dst, dead):
    at = src
    if (src ^ dst) & 1:
        if [src, DIE] in dead["mate_links"] or [src ^ 1, DIE] in dead["mate_links"] or (src ^ 1) in dead["chips"]:
            return False
        at = src ^ 1
    if at != dst and ([at, DIE] in dead["switch_ports"] or [dst, DIE] in dead["switch_ports"]):
        return False
    return dst not in dead["chips"]


def build():
    a1, a2, a3, a4, e, b3, b2, b1 = RING
    par = [{}, {}]

    def link(f, seq):
        for i in range(len(seq) - 1):
            par[f][seq[i]] = seq[i + 1]

    link(0, [a1, a2, a3, a4, e, PATH[5]])
    link(0, [b1, b2, b3, e])
    link(0, PATH + [GATE, ROOT])
    link(1, [e, b3, b2, b1, a1, PATH[0]])
    link(1, [a4, a3, a2, a1])
    link(1, PATH[::-1] + [GATE, ROOT])
    chips = RING + PATH + [GATE, ROOT]
    kids = [{v: [c for c in chips if par[f].get(c) == v] for v in chips} for f in (0, 1)]
    for f in (0, 1):
        for v in chips:
            kids[f][v].sort(key=lambda c: c != ADD_TO.get(v))
    both = {a2: 0, b3: 1}

    slot = {}
    tenants = {}
    for v in chips:
        late = 0 if (v, 0) in CROSS else 1
        order = [(0, 0), (1, 0), (1 - late, 1), (late, 1)]
        for f in (0, 1):
            if both.get(v) == f or (v != ROOT and not kids[f][v]):
                order = [(f, 0), (f, 1), (1 - f, 0), (1 - f, 1)]
        for f, j in order:
            for c in (kids[f][v] or [None]):
                s = f
                if v in both:
                    s = j
                elif c is not None and len(kids[f][v]) == 2 and par[1 - f][v] == c:
                    s = 1 - f
                elif c is not None and j == 1 and (v, f) in CROSS:
                    s = 1 - f
                slot[(v, f, j, c)] = s
                tenants.setdefault((v, s), []).append((f, j, c))

    need = {}
    after = {}
    ncred = {}

    def dep(op, what, on):
        need.setdefault(op, []).append(what)
        after.setdefault(op, []).append(on)

    for (v, s), seq in sorted(tenants.items()):
        landed = 0
        loaded = 0
        for i, (f, j, c) in enumerate(seq):
            before = seq[i - 1] if i else None
            if c is not None:
                landed += 8
            if v != ROOT and (c is None or c == kids[f][v][0]):
                loaded += 16
                need.setdefault(('L', v, f, j), [])
                after.setdefault(('L', v, f, j), [])
                dep(('D', v, f, j), ('ld', s, loaded), ('L', v, f, j))
                if c is not None:
                    dep(('L', v, f, j), ('arr', s, landed), ('D', c, f, j))
                elif before:
                    dep(('L', v, f, j), ('sent',), ('D', v, before[0], before[1]))
            elif v != ROOT:
                dep(('D', v, f, j), ('arr', s, landed), ('D', c, f, j))
            if c is None or not before:
                continue
            reader = ('D', v, before[0], before[1])
            if v != ROOT and par[before[0]][v] == c:
                sc = slot[(c, before[0], before[1], v)]
                k = tenants[(c, sc)].index((before[0], before[1], v))
                n = 8 * len([t for t in tenants[(c, sc)][:k + 1] if t[2] is not None])
                dep(('D', c, f, j), ('arr', sc, n), reader)
            elif v == ROOT:
                sig = ('K', v, c, 0, j)
                dep(('D', c, f, j), ('cr', 0, 1), sig)
                dep(sig, ('root',), ('D', c, before[0], before[1]))
            else:
                sig = ('K', v, c, f, j)
                ncred[(c, f)] = ncred.get((c, f), 0) + 1
                dep(('D', c, f, j), ('cr', f, ncred[(c, f)]), sig)
                dep(sig, ('sent',), reader)

    ready = {}

    def chain(op):
        if op not in ready:
            got = [chain(o) for o in after[op]] + [(0, 0)]
            ready[op] = (max(w for w, s in got), max(s for w, s in got) + (1 if op[1] == ROOT else 0))
        w, s = ready[op]
        return (w + (op[0] != 'L'), s + 1)

    for op in list(after):
        chain(op)
    return par, kids, slot, need, ready


def rank_program(g, core, T, topo):
    if T.rank_of(core) is None:
        return
    par, kids, slot, need, ready = build()
    me = 16 * topo.host(core) + topo.chip(core)
    arr = [T.sem.arr0, T.sem.arr1]
    cr = [T.sem.crA, T.sem.crB]
    ld = [T.sem.ld0, T.sem.ld1]
    n = {"sent": 0}
    seen = {}

    def wait(key, sem, count):
        if seen.get(key, 0) < count:
            g.wait_ge(sem, count)
            seen[key] = count

    def local(out, in_, add, sem):
        if add:
            g.dma_start(out, in_, accum_op=AluOpType.add, max_dma_last_dim=8192).then_inc(sem, 16)
        else:
            g.dma_start(out, in_).then_inc(sem, 16)

    def address(chip):
        if not alive(me, chip, T.tables["DEAD"]):
            raise ValueError("the plan's write from chip %d to chip %d crosses a dead part" % (me, chip))
        return topo.addr(world(chip), core)

    def signal(targets):
        trs = []
        for i, (chip, f) in enumerate(targets):
            rid, pid = address(chip)
            trs.append(RemoteDMATransfer(dst_ids=[DstId(rid=rid, pnc=pid)], dma_engine_mask=1 << i, remote_sem=cr[f]))
        g.remote_dma_fused(trs, local_sem=T.sem.sent)
        n["sent"] += len(targets)

    if me == ROOT:
        local(T.y[:], T.x[:], False, ld[0])
        wait("ld0", ld[0], 16)
        for j in (0, 1):
            wait("arr0", arr[0], 8 * (j + 1))
            wait("arr1", arr[1], 8 * (j + 1))
            local(T.y[4 * j:4 * j + 4], T.buf[:], True, ld[0])
            wait("ld0", ld[0], 16 * (j + 2))
            if j == 0:
                signal([(GATE, 0)])
        wait("sent", T.sem.sent, n["sent"])
        return

    mine = sorted((r, op) for op, r in ready.items() if op[1] == me)
    for t in sorted({r[0] for r, op in mine}):
        ops = [op for r, op in mine if r[0] == t]
        if [op for op in ops if ('sent',) in need[op]]:
            wait("sent", T.sem.sent, n["sent"])
        sigs = [(op[2], op[3]) for op in ops if op[0] == 'K']
        if sigs:
            signal(sigs)
        for op in ops:
            if op[0] == 'K':
                continue
            for w in need[op]:
                if w[0] == 'arr':
                    wait("arr%d" % w[1], arr[w[1]], w[2])
                elif w[0] == 'cr':
                    wait("cr%d" % w[1], cr[w[1]], w[2])
                elif w[0] == 'ld':
                    wait("ld%d" % w[1], ld[w[1]], w[2])
            k, v, f, j = op
            cs = kids[f][me]
            mine_in = [slot[(me, f, j, c)] for c in (cs or [None])]
            if k == 'L':
                local(T.buf[mine_in[0]], T.x[4 * j + 2 * f:4 * j + 2 * f + 2], bool(cs), ld[mine_in[0]])
                continue
            p = par[f][me]
            s = slot[(p, f, j, me)]
            rid, pid = address(p)
            if len(cs) == 2:
                g.remote_dma_fused([RemoteDMATransfer(
                    dst_ids=[DstId(rid=rid, pnc=pid)], dma_engine_mask=DATA_ENGINES, remote_sem=arr[s],
                    srcs=[T.buf[i] for i in mine_in], dsts=[T.buf[s]], alu_op=1)], local_sem=T.sem.sent)
            else:
                g.remote_dma(T.buf[s], T.buf[mine_in[0]], arr[s], T.sem.sent, pid, rid, DATA_ENGINES)
            n["sent"] += 8
    wait("sent", T.sem.sent, n["sent"])
